import numpy as np
import ml_dtypes


def mxq(x, axis, fmt="e4m3"):
    dtype, down = {"e4m3": (ml_dtypes.float8_e4m3fn, 7), "e5m2": (ml_dtypes.float8_e5m2, 14)}[fmt]
    v = np.moveaxis(np.asarray(x, np.float32).astype(ml_dtypes.bfloat16).astype(np.float64), axis, -1)
    blocks = v.reshape(v.shape[:-1] + (-1, 32))
    amax = np.abs(blocks).max(-1, keepdims=True)
    byte = np.maximum(np.where(amax > 0, np.frexp(amax)[1] - 1 + 127, 0) - down, 1)
    scale = np.exp2(byte - 127.0)
    codes = (blocks / scale).astype(np.float32).astype(dtype).astype(np.float64)
    return np.moveaxis((codes * scale).reshape(v.shape), -1, axis)


WIDE = False


def mx_kscale(k):
    if not WIDE:
        return np.ones(k)
    levels = np.array([24, -24, 12, -12, 0])
    if k % 512:
        return np.exp2(np.random.permutation(np.resize(levels, k // 32))).repeat(32)
    a = np.empty((k // 512, 16))
    for p in range(k // 512):
        a[p, :8] = np.random.permutation(np.resize(levels, 8))
        for g in range(8):
            far = levels[np.abs(levels - a[p, g]) >= 10]
            a[p, g + 8] = far[np.random.randint(len(far))]
    return np.exp2(a.ravel()).repeat(32)


def f64(x):
    return np.asarray(x).astype(np.float64)


def striped8(idx):
    return np.concatenate([v.reshape(-1, 16).T for v in idx]).astype(np.uint16)


def unstriped8(offs):
    return np.stack([offs[16 * g:16 * g + 16].T.reshape(-1) for g in range(8)]).astype(np.int64)


E2M1 = np.array([0.0, 0.5, 1.0, 1.5, 2.0, 3.0, 4.0, 6.0, -0.0, -0.5, -1.0, -1.5, -2.0, -3.0, -4.0, -6.0])


def pack_weight(w, fmt):
    k, n = w.shape
    w = f64(np.asarray(w, np.float32).astype(ml_dtypes.bfloat16)).reshape(k // 32, 32, n)
    amax = np.abs(w).max(1)
    if fmt == "e4m3":
        byte = np.frexp(amax)[1] - 1 + 127 - 7
    else:
        mant, ex = np.frexp(amax / 6.0)
        byte = np.where(mant > 0.5, ex, ex - 1) + 127
    byte = np.clip(np.where(amax > 0, byte, 1), 1, 254)
    scaled = (w * np.exp2(127.0 - byte)[:, None, :]).reshape(k, n).astype(np.float32)
    by_word = np.ascontiguousarray(scaled.reshape(k // 512, 128, 4, n).transpose(0, 1, 3, 2))
    if fmt == "e4m3":
        words = by_word.astype(ml_dtypes.float8_e4m3fn).view(np.uint8)
    else:
        c = by_word.astype(ml_dtypes.float4_e2m1fn).view(np.uint8) & 0xF
        words = (c[..., 0::2] | (c[..., 1::2] << 4)).reshape(k // 512, 128, 2 * n)
    return np.ascontiguousarray(words), np.ascontiguousarray(byte.astype(np.uint8).reshape(k // 512, 16, n))


def unpack_weight(words, scales, fmt):
    g, _, n = scales.shape
    words = np.ascontiguousarray(words).reshape(g, 128, n, -1)
    if fmt == "e4m3":
        vals = words.view(ml_dtypes.float8_e4m3fn).astype(np.float64)
    else:
        nib = np.empty((g, 128, n, 4), np.uint8)
        nib[..., 0::2] = words & 0xF
        nib[..., 1::2] = words >> 4
        vals = E2M1[nib]
    vals = vals * np.repeat(np.exp2(scales.astype(np.float64) - 127.0), 8, axis=1)[..., None]
    return vals.transpose(0, 1, 3, 2).reshape(g * 512, n)


def planes(y):
    n, m = y.shape
    v = y.astype(np.float32).astype(ml_dtypes.bfloat16).astype(np.float64).reshape(n // 32, 32, m)
    top = np.abs(v).max(1)
    byte = np.clip(np.where(top > 0, np.frexp(top)[1] - 1 + 127 - 7, 1), 1, 254)
    codes = (v * np.exp2(127.0 - byte)[:, None, :]).reshape(n, m).astype(np.float32).astype(ml_dtypes.float8_e4m3fn).view(np.uint8)
    words = codes.reshape(n // 512, 128, 4, m).transpose(0, 1, 3, 2)
    return np.ascontiguousarray(words), np.ascontiguousarray(byte.astype(np.uint8).reshape(n // 512, 16, m))


K, L, N, T, J = 512, 512, 512, 2048, 1024


def setup_inputs():
    n = np.random.standard_normal
    s = mx_kscale(K)[:, None]
    s2 = mx_kscale(L)[:, None]
    p_wa = pack_weight(n((K, N)) / np.sqrt(K) / s, "e4m3")
    p_wb = pack_weight(n((L, N)) / np.sqrt(L) / s2, "e4m3")
    return {
        "xT": (n((K, T)) * s).astype(np.float32),
        "wgt": np.repeat(np.random.uniform(0.5, 2.0, (8, J)), 16, axis=0).astype(np.float32),
        "zT": (n((L, T)) * s2).astype(np.float32),
        "wgt2": np.repeat(np.random.uniform(0.5, 2.0, (8, J)), 16, axis=0).astype(np.float32),
        "wa_words": p_wa[0],
        "wa_scales": p_wa[1],
        "wb_words": p_wb[0],
        "wb_scales": p_wb[1],
        "offs": striped8(np.stack([np.random.permutation(T)[:J] for _ in range(8)])),
        "offs2": striped8(np.stack([np.random.permutation(T)[:J] for _ in range(8)])),
    }


def reference(xT, wgt, zT, wgt2, wa_words, wa_scales, wb_words, wb_scales, offs, offs2):
    idx = unstriped8(offs)
    idx2 = unstriped8(offs2)
    rows = np.arange(K)
    xg = f64(wgt)[rows // 4 % 128] * f64(xT)[rows[:, None], idx[rows % 512 // 64]]
    xT_ = mxq(xg, 0, "e4m3")
    rows = np.arange(L)
    xg = f64(wgt2)[rows // 4 % 128] * f64(zT)[rows[:, None], idx2[rows % 512 // 64]]
    zT_ = mxq(xg, 0, "e4m3")
    wa_ = unpack_weight(wa_words, wa_scales, "e4m3")
    wb_ = unpack_weight(wb_words, wb_scales, "e4m3")
    y = wa_.T @ xT_ + wb_.T @ zT_
    return (y,) + planes(y)

@@ -1,0 +1,176 @@
+from contextlib import ExitStack
+
+import concourse.mybir as mybir
+
+K, L, N, T, J = 512, 512, 512, 2048, 1024
+FLOPS = 2 * (K + L) * N * J
+
+F32 = mybir.dt.float32
+BF16 = mybir.dt.bfloat16
+I32 = mybir.dt.int32
+U16 = mybir.dt.uint16
+U8 = mybir.dt.uint8
+FP8X4 = mybir.dt.float8_e4m3fn_x4
+MULT = mybir.AluOpType.mult
+
+P = 128
+PACK = 4
+BANK_J = 128
+CHUNK = 256
+LIST_ROWS = 16
+
+
+def tile_list_sum_noneP_kernel(
+    tc, xT, wgt, zT, wgt2, wa_words, wa_scales, wb_words, wb_scales, offs, offs2, out_0, out_1, out_2
+):
+    nc = tc.nc
+    n_chunks = J // CHUNK
+    with ExitStack() as ctx:
+        keep = ctx.enter_context(tc.tile_pool(name="keep", bufs=1))
+        psum = ctx.enter_context(tc.psum_pool(name="psum", bufs=1))
+
+        x_rows = xT.rearrange("(p i) t -> p i t", i=PACK)
+        z_rows = zT.rearrange("(p i) t -> p i t", i=PACK)
+        x_planes = [keep.tile([P, T], F32, name="x_plane%d" % i) for i in range(PACK)]
+        z_planes = [keep.tile([P, T], F32, name="z_plane%d" % i) for i in range(PACK)]
+        x_list = keep.tile([P, J // LIST_ROWS], U16, name="x_list")
+        z_list = keep.tile([P, J // LIST_ROWS], U16, name="z_list")
+        x_gain = keep.tile([P, J], F32, name="x_gain")
+        z_gain = keep.tile([P, J], F32, name="z_gain")
+        wa_raw = keep.tile([P, N], I32, name="wa_raw")
+        wb_raw = keep.tile([P, N], I32, name="wb_raw")
+        ws_raw = keep.tile([P, N], U8, name="ws_raw")
+
+        nc.gpsimd.memset(ws_raw[:].bitcast(I32), 0)
+        for q in range(4):
+            nc.gpsimd.dma_start(
+                out=ws_raw[32 * q : 32 * q + 4, :].bitcast(I32), in_=wa_scales[0, 4 * q : 4 * q + 4, :].bitcast(I32)
+            )
+            nc.gpsimd.dma_start(
+                out=ws_raw[32 * q + 4 : 32 * q + 8, :].bitcast(I32), in_=wb_scales[0, 4 * q : 4 * q + 4, :].bitcast(I32)
+            )
+
+        nc.sync.dma_start(out=x_planes[0][:], in_=x_rows[:, 0, :])
+        nc.sync.dma_start(x_list[:], offs)
+        nc.sync.dma_start(out=x_gain[:], in_=wgt)
+        for i in range(1, PACK):
+            nc.sync.dma_start(out=x_planes[i][:], in_=x_rows[:, i, :])
+        nc.sync.dma_start(out=wa_raw[:], in_=wa_words[0].rearrange("p n i -> p (n i)").bitcast(I32))
+        nc.sync.dma_start(out=wb_raw[:], in_=wb_words[0].rearrange("p n i -> p (n i)").bitcast(I32))
+        nc.sync.dma_start(z_list[:], offs2)
+        nc.sync.dma_start(out=z_gain[:], in_=wgt2)
+        for i in range(PACK):
+            nc.sync.dma_start(out=z_planes[i][:], in_=z_rows[:, i, :])
+
+        x_picked = keep.tile([P, PACK, J], F32, name="x_picked")
+        z_picked = keep.tile([P, PACK, J], F32, name="z_picked")
+
+        def gather(picked, planes, offsets, gain, i, j0, j1):
+            nc.vector.tensor_tensor(
+                picked[:, i, j0:j1],
+                planes[i][:].indirect(offsets[:, j0 // LIST_ROWS : j1 // LIST_ROWS]),
+                gain[:, j0:j1],
+                MULT,
+            )
+
+        def quantise(woven, name):
+            width = woven.shape[1]
+            codes = keep.tile([P, width], I32, name=name + "_codes", align_bytes=64)
+            scales = keep.tile([P, width], U8, name=name + "_scales", align_bytes=64)
+            nc.vector.quantize_mx(
+                out=codes[:].bitcast(FP8X4), scales=scales[:], in_=woven[:].rearrange("p j i -> p (j i)")
+            )
+            return codes, scales
+
+        banks = [psum.tile([P, PACK, BANK_J], F32, name="bank%d" % b) for b in range(J // BANK_J)]
+        wa_dealt = keep.tile([P, PACK, P], I32, name="wa_dealt", align_bytes=64)
+        wb_dealt = keep.tile([P, PACK, P], I32, name="wb_dealt", align_bytes=64)
+        ws_dealt = keep.tile([P, PACK, P], U8, name="ws_dealt", align_bytes=64)
+
+        def passes(c, w_dealt, first_scale_row, codes, scales, opens):
+            for h in range(CHUNK // BANK_J):
+                cols = slice(h * BANK_J, (h + 1) * BANK_J)
+                for t in range(PACK):
+                    nc.tensor.matmul_mx(
+                        out=banks[c * (CHUNK // BANK_J) + h][:, t, :],
+                        lhsT=w_dealt[:, t, :].bitcast(FP8X4),
+                        lhsT_scale=ws_dealt[first_scale_row:P, t, :],
+                        rhs=codes[:, cols].bitcast(FP8X4),
+                        rhs_scale=scales[:, cols],
+                        start=(opens and t == 0),
+                        stop=(not opens and t == PACK - 1),
+                    )
+
+        for i in range(PACK - 1):
+            gather(x_picked, x_planes, x_list, x_gain, i, 0, J)
+        x_woven = [keep.tile([P, CHUNK, PACK], BF16, name="x_woven%d" % c, align_bytes=64) for c in range(n_chunks)]
+        for c in range(n_chunks):
+            j0, j1 = c * CHUNK, (c + 1) * CHUNK
+            gather(x_picked, x_planes, x_list, x_gain, PACK - 1, j0, j1)
+            nc.scalar.copy(
+                out=x_woven[c][:].rearrange("p (c r) i -> p c i r", r=4),
+                in_=x_picked[:, :, j0:j1].rearrange("p i (c r) -> p c i r", r=4),
+            )
+        nc.vector.tensor_copy(out=wa_dealt[:], in_=wa_raw[:].rearrange("p (m t) -> p t m", t=PACK))
+        nc.vector.tensor_copy(out=ws_dealt[:], in_=ws_raw[:].rearrange("p (m t) -> p t m", t=PACK))
+        nc.vector.tensor_copy(out=wb_dealt[:], in_=wb_raw[:].rearrange("p (m t) -> p t m", t=PACK))
+        for c in range(n_chunks):
+            codes, scales = quantise(x_woven[c], "x%d" % c)
+            passes(c, wa_dealt, 0, codes, scales, True)
+
+        z_woven = [keep.tile([P, CHUNK, PACK], BF16, name="z_woven%d" % c, align_bytes=64) for c in range(n_chunks)]
+
+        def weave_pair(c, i0):
+            nc.scalar.copy(
+                out=z_woven[c][:, :, i0 : i0 + 2],
+                in_=z_picked[:, i0 : i0 + 2, c * CHUNK : (c + 1) * CHUNK].rearrange("p i j -> p j i"),
+            )
+
+        for i in range(2):
+            gather(z_picked, z_planes, z_list, z_gain, i, 0, J)
+        for c in range(n_chunks):
+            weave_pair(c, 0)
+        gather(z_picked, z_planes, z_list, z_gain, 2, 0, J)
+
+        y_rows = out_0.rearrange("(p t) j -> p t j", t=PACK)
+        y_words = out_1[0].rearrange("p j i -> p (j i)").bitcast(I32)
+        y_scales = keep.tile([P, J], U8, name="y_scales", align_bytes=64)
+
+        def front(c):
+            gather(z_picked, z_planes, z_list, z_gain, PACK - 1, c * CHUNK, (c + 1) * CHUNK)
+            weave_pair(c, 2)
+
+        def middle(c):
+            codes, scales = quantise(z_woven[c], "z%d" % c)
+            passes(c, wb_dealt, 4, codes, scales, False)
+            y = keep.tile([P, PACK, CHUNK], F32, name="y%d" % c)
+            for h in range(CHUNK // BANK_J):
+                nc.scalar.copy(out=y[:, :, h * BANK_J : (h + 1) * BANK_J], in_=banks[c * (CHUNK // BANK_J) + h][:])
+            nc.sync.dma_start(out=y_rows[:, :, c * CHUNK : (c + 1) * CHUNK], in_=y[:])
+            return y
+
+        def back(c, y):
+            cols = slice(c * CHUNK, (c + 1) * CHUNK)
+            y_woven = keep.tile([P, CHUNK, PACK], BF16, name="y_woven%d" % c, align_bytes=64)
+            nc.vector.tensor_copy(
+                out=y_woven[:].rearrange("p (c r) t -> p c t r", r=4),
+                in_=y[:].rearrange("p t (c r) -> p c t r", r=4),
+            )
+            y_codes = keep.tile([P, CHUNK], I32, name="y_codes%d" % c, align_bytes=64)
+            nc.vector.quantize_mx(
+                out=y_codes[:].bitcast(FP8X4), scales=y_scales[:, cols], in_=y_woven[:].rearrange("p j t -> p (j t)")
+            )
+            nc.sync.dma_start(out=y_words[:, cols], in_=y_codes[:])
+
+        ys = {}
+        for s in range(n_chunks + 2):
+            if s < n_chunks:
+                front(s)
+            if 1 <= s <= n_chunks:
+                ys[s - 1] = middle(s - 1)
+            if s >= 2:
+                back(s - 2, ys[s - 2])
+        for q in range(4):
+            nc.sync.dma_start(
+                out=out_2[0, 4 * q : 4 * q + 4, :].bitcast(I32), in_=y_scales[32 * q : 32 * q + 4, :].bitcast(I32)
+            )

@@ -1,6 +1,7 @@
 from contextlib import ExitStack
 
 import concourse.mybir as mybir
+from concourse.masks import make_identity
 
 K, L, N, T, J = 512, 512, 512, 2048, 1024
 FLOPS = 2 * (K + L) * N * J
@@ -16,15 +17,21 @@ MULT = mybir.AluOpType.mult
 P = 128
 PACK = 4
 BANK_J = 128
-CHUNK = 256
+X_CHUNK = 256
+Z_GROUPS = ((128, 256, 256), (256,), (128,))
+SCALAR_ROUNDS = (0, 1)
+VECTOR_WEAVES = (0, 3, 4)
+HOLD = 3
+X_STEPS = ((0, 1), (1, 2), (2, 4))
 LIST_ROWS = 16
+QUADS = 4
+HEADS = 8
 
 
 def tile_list_sum_noneP_kernel(
     tc, xT, wgt, zT, wgt2, wa_words, wa_scales, wb_words, wb_scales, offs, offs2, out_0, out_1, out_2
 ):
     nc = tc.nc
-    n_chunks = J // CHUNK
     with ExitStack() as ctx:
         keep = ctx.enter_context(tc.tile_pool(name="keep", bufs=1))
         psum = ctx.enter_context(tc.psum_pool(name="psum", bufs=1))
@@ -37,40 +44,76 @@ def tile_list_sum_noneP_kernel(
         z_list = keep.tile([P, J // LIST_ROWS], U16, name="z_list")
         x_gain = keep.tile([P, J], F32, name="x_gain")
         z_gain = keep.tile([P, J], F32, name="z_gain")
-        wa_raw = keep.tile([P, N], I32, name="wa_raw")
-        wb_raw = keep.tile([P, N], I32, name="wb_raw")
+        x_gain_rows = keep.tile([P, J // QUADS], F32, name="x_gain_rows")
+        z_gain_rows = keep.tile([P, J // QUADS], F32, name="z_gain_rows")
+        w_raw = keep.tile([P, 2, N], I32, name="w_raw")
         ws_raw = keep.tile([P, N], U8, name="ws_raw")
+        identity = keep.tile([P, P], F32, name="identity")
 
-        nc.gpsimd.memset(ws_raw[:].bitcast(I32), 0)
-        for q in range(4):
-            nc.gpsimd.dma_start(
-                out=ws_raw[32 * q : 32 * q + 4, :].bitcast(I32), in_=wa_scales[0, 4 * q : 4 * q + 4, :].bitcast(I32)
-            )
-            nc.gpsimd.dma_start(
-                out=ws_raw[32 * q + 4 : 32 * q + 8, :].bitcast(I32), in_=wb_scales[0, 4 * q : 4 * q + 4, :].bitcast(I32)
-            )
+        nc.vector.memset(ws_raw[:].bitcast(I32), 0)
+        make_identity(nc, identity[:])
 
-        nc.sync.dma_start(out=x_planes[0][:], in_=x_rows[:, 0, :])
+        def load_scale_rows(q):
+            for first, scales in ((0, wa_scales), (4, wb_scales)):
+                nc.sync.dma_start(
+                    out=ws_raw[32 * q + first : 32 * q + first + 4, :].bitcast(I32),
+                    in_=scales[0, 4 * q : 4 * q + 4, :].bitcast(I32),
+                )
+
+        def load_gain_rows(rows, gain_hbm):
+            width = J // QUADS
+            for q in range(QUADS):
+                nc.sync.dma_start(out=rows[32 * q : 32 * q + 32, :], in_=gain_hbm[0:P:4, q * width : (q + 1) * width])
+
+        load_gain_rows(x_gain_rows, wgt)
         nc.sync.dma_start(x_list[:], offs)
-        nc.sync.dma_start(out=x_gain[:], in_=wgt)
-        for i in range(1, PACK):
-            nc.sync.dma_start(out=x_planes[i][:], in_=x_rows[:, i, :])
-        nc.sync.dma_start(out=wa_raw[:], in_=wa_words[0].rearrange("p n i -> p (n i)").bitcast(I32))
-        nc.sync.dma_start(out=wb_raw[:], in_=wb_words[0].rearrange("p n i -> p (n i)").bitcast(I32))
+        nc.sync.dma_start(out=x_planes[0][:], in_=x_rows[:, 0, :])
+        nc.sync.dma_start(out=x_planes[1][:], in_=x_rows[:, 1, :])
+        load_gain_rows(z_gain_rows, wgt2)
+        nc.sync.dma_start(out=x_planes[2][:], in_=x_rows[:, 2, :])
+        load_scale_rows(0)
+        nc.sync.dma_start(out=x_planes[3][:], in_=x_rows[:, 3, :])
+        load_scale_rows(1)
+        load_scale_rows(2)
+        nc.sync.dma_start(out=w_raw[:, 0, :], in_=wa_words[0].rearrange("p n i -> p (n i)").bitcast(I32))
+        nc.sync.dma_start(out=w_raw[:, 1, :], in_=wb_words[0].rearrange("p n i -> p (n i)").bitcast(I32))
+        nc.sync.dma_start(out=z_planes[0][:], in_=z_rows[:, 0, :])
         nc.sync.dma_start(z_list[:], offs2)
-        nc.sync.dma_start(out=z_gain[:], in_=wgt2)
-        for i in range(PACK):
+        load_scale_rows(3)
+        for i in range(1, PACK):
             nc.sync.dma_start(out=z_planes[i][:], in_=z_rows[:, i, :])
 
-        x_picked = keep.tile([P, PACK, J], F32, name="x_picked")
-        z_picked = keep.tile([P, PACK, J], F32, name="z_picked")
+        def spread_gain(rows, gain, name, steps):
+            blocks = J // QUADS // P
+            turned = psum.tile([P, blocks, P], F32, name=name + "_turned", tag="bank7")
+            for b in range(blocks):
+                nc.tensor.transpose(turned[:, b, :], rows[:, b * P : (b + 1) * P], identity[:])
+            by_place = turned[:].rearrange("p b (q g s) -> p q b g s", q=QUADS, g=HEADS)
+            for q0, q1 in steps:
+                wide = keep.tile([P, q1 - q0, blocks, HEADS, LIST_ROWS], F32, name=name + "_wide%d" % q0)
+                nc.scalar.copy(
+                    out=wide[:],
+                    in_=by_place[:, q0:q1, :, :, 0:1].to_broadcast([P, q1 - q0, blocks, HEADS, LIST_ROWS]),
+                )
+                back = psum.tile([P, (q1 - q0) * blocks, P], F32, name=name + "_back%d" % q0, tag="bank%d" % (3 + q0))
+                flat = wide[:].rearrange("p q b g s -> p (q b) (g s)")
+                for u in range((q1 - q0) * blocks):
+                    nc.tensor.transpose(back[:, u, :], flat[:, u, :], identity[:])
+                nc.scalar.copy(
+                    out=gain[:, q0 * (J // QUADS) : q1 * (J // QUADS)], in_=back[:].rearrange("p u r -> p (u r)")
+                )
 
-        def gather(picked, planes, offsets, gain, i, j0, j1):
+        spread_gain(x_gain_rows, x_gain, "x_gain", X_STEPS)
+        spread_gain(z_gain_rows, z_gain, "z_gain", ((0, 2), (2, 4)))
+
+        def gather(picked, plane, offsets, gain, j0, j1):
             nc.vector.tensor_tensor(
-                picked[:, i, j0:j1],
-                planes[i][:].indirect(offsets[:, j0 // LIST_ROWS : j1 // LIST_ROWS]),
-                gain[:, j0:j1],
-                MULT,
+                picked, plane[:].indirect(offsets[:, j0 // LIST_ROWS : j1 // LIST_ROWS]), gain[:, j0:j1], MULT
+            )
+
+        def weave(engine_copy, woven, planes):
+            engine_copy(
+                out=woven.rearrange("p (c r) i -> p c i r", r=4), in_=planes.rearrange("p i (c r) -> p c i r", r=4)
             )
 
         def quantise(woven, name):
@@ -82,95 +125,109 @@ def tile_list_sum_noneP_kernel(
             )
             return codes, scales
 
-        banks = [psum.tile([P, PACK, BANK_J], F32, name="bank%d" % b) for b in range(J // BANK_J)]
-        wa_dealt = keep.tile([P, PACK, P], I32, name="wa_dealt", align_bytes=64)
-        wb_dealt = keep.tile([P, PACK, P], I32, name="wb_dealt", align_bytes=64)
+        banks = [psum.tile([P, PACK, BANK_J], F32, name="bank%d" % b, tag="bank%d" % b) for b in range(J // BANK_J)]
+        w_dealt = keep.tile([P, 2, PACK, P], I32, name="w_dealt", align_bytes=64)
         ws_dealt = keep.tile([P, PACK, P], U8, name="ws_dealt", align_bytes=64)
 
-        def passes(c, w_dealt, first_scale_row, codes, scales, opens):
-            for h in range(CHUNK // BANK_J):
-                cols = slice(h * BANK_J, (h + 1) * BANK_J)
+        def passes(j0, j1, stream, codes, scales):
+            for b0 in range(j0, j1, BANK_J):
+                cols = slice(b0 - j0, b0 - j0 + BANK_J)
                 for t in range(PACK):
                     nc.tensor.matmul_mx(
-                        out=banks[c * (CHUNK // BANK_J) + h][:, t, :],
-                        lhsT=w_dealt[:, t, :].bitcast(FP8X4),
-                        lhsT_scale=ws_dealt[first_scale_row:P, t, :],
+                        out=banks[b0 // BANK_J][:, t, :],
+                        lhsT=w_dealt[:, stream, t, :].bitcast(FP8X4),
+                        lhsT_scale=ws_dealt[4 * stream : P, t, :],
                         rhs=codes[:, cols].bitcast(FP8X4),
                         rhs_scale=scales[:, cols],
-                        start=(opens and t == 0),
-                        stop=(not opens and t == PACK - 1),
+                        start=(stream == 0 and t == 0),
+                        stop=(stream == 1 and t == PACK - 1),
                     )
 
-        for i in range(PACK - 1):
-            gather(x_picked, x_planes, x_list, x_gain, i, 0, J)
-        x_woven = [keep.tile([P, CHUNK, PACK], BF16, name="x_woven%d" % c, align_bytes=64) for c in range(n_chunks)]
-        for c in range(n_chunks):
-            j0, j1 = c * CHUNK, (c + 1) * CHUNK
-            gather(x_picked, x_planes, x_list, x_gain, PACK - 1, j0, j1)
-            nc.scalar.copy(
-                out=x_woven[c][:].rearrange("p (c r) i -> p c i r", r=4),
-                in_=x_picked[:, :, j0:j1].rearrange("p i (c r) -> p c i r", r=4),
-            )
-        nc.vector.tensor_copy(out=wa_dealt[:], in_=wa_raw[:].rearrange("p (m t) -> p t m", t=PACK))
+        x_picked = keep.tile([P, PACK, J], F32, name="x_picked")
+        for q0, q1 in X_STEPS:
+            j0, j1 = q0 * (J // QUADS), q1 * (J // QUADS)
+            gather(x_picked[:, 0, j0:j1], x_planes[0], x_list, x_gain, j0, j1)
+        for i in range(1, PACK - 1):
+            gather(x_picked[:, i, :], x_planes[i], x_list, x_gain, 0, J)
+        nc.vector.tensor_copy(
+            out=w_dealt[:].rearrange("p w t (a r) -> p w a t r", r=4),
+            in_=w_raw[:].rearrange("p w (a r t) -> p w a t r", r=4, t=PACK),
+        )
+        x_woven = {}
+        for j0 in range(0, J, X_CHUNK):
+            j1 = j0 + X_CHUNK
+            gather(x_picked[:, PACK - 1, j0:j1], x_planes[PACK - 1], x_list, x_gain, j0, j1)
+            x_woven[j0] = keep.tile([P, X_CHUNK, PACK], BF16, name="x_woven%d" % j0, align_bytes=64)
+            weave(nc.scalar.copy, x_woven[j0][:], x_picked[:, :, j0:j1])
         nc.vector.tensor_copy(out=ws_dealt[:], in_=ws_raw[:].rearrange("p (m t) -> p t m", t=PACK))
-        nc.vector.tensor_copy(out=wb_dealt[:], in_=wb_raw[:].rearrange("p (m t) -> p t m", t=PACK))
-        for c in range(n_chunks):
-            codes, scales = quantise(x_woven[c], "x%d" % c)
-            passes(c, wa_dealt, 0, codes, scales, True)
+        for j0 in range(0, J, X_CHUNK):
+            codes, scales = quantise(x_woven[j0], "x%d" % j0)
+            passes(j0, j0 + X_CHUNK, 0, codes, scales)
 
-        z_woven = [keep.tile([P, CHUNK, PACK], BF16, name="z_woven%d" % c, align_bytes=64) for c in range(n_chunks)]
-
-        def weave_pair(c, i0):
-            nc.scalar.copy(
-                out=z_woven[c][:, :, i0 : i0 + 2],
-                in_=z_picked[:, i0 : i0 + 2, c * CHUNK : (c + 1) * CHUNK].rearrange("p i j -> p j i"),
-            )
-
-        for i in range(2):
-            gather(z_picked, z_planes, z_list, z_gain, i, 0, J)
-        for c in range(n_chunks):
-            weave_pair(c, 0)
-        gather(z_picked, z_planes, z_list, z_gain, 2, 0, J)
+        widths = [w for group in Z_GROUPS for w in group]
+        bounds = [sum(widths[:c]) for c in range(len(widths) + 1)]
+        n_chunks = len(widths)
+        group_of = [g for g, group in enumerate(Z_GROUPS) for w in group]
+        z_woven = {}
+        z_picked = {}
 
         y_rows = out_0.rearrange("(p t) j -> p t j", t=PACK)
         y_words = out_1[0].rearrange("p j i -> p (j i)").bitcast(I32)
         y_scales = keep.tile([P, J], U8, name="y_scales", align_bytes=64)
 
         def front(c):
-            gather(z_picked, z_planes, z_list, z_gain, PACK - 1, c * CHUNK, (c + 1) * CHUNK)
-            weave_pair(c, 2)
+            g = group_of[c]
+            first = group_of.index(g)
+            g0, g1 = bounds[first], bounds[first] + sum(Z_GROUPS[g])
+            j0, j1 = bounds[c], bounds[c + 1]
+            if c == first:
+                tag = "z_woven%d" % (c - HOLD) if g > 0 else "z_first"
+                z_picked[g] = keep.tile([P, PACK, g1 - g0], F32, name="z_picked%d" % g, tag=tag, align_bytes=64)
+                for i in range(PACK - 1):
+                    gather(z_picked[g][:, i, :], z_planes[i], z_list, z_gain, g0, g1)
+            gather(z_picked[g][:, PACK - 1, j0 - g0 : j1 - g0], z_planes[PACK - 1], z_list, z_gain, j0, j1)
+            z_woven[c] = keep.tile([P, j1 - j0, PACK], BF16, name="z_woven%d" % c, tag="z_woven%d" % c, align_bytes=64)
+            weave(nc.vector.tensor_copy if c in VECTOR_WEAVES else nc.scalar.copy, z_woven[c][:], z_picked[g][:, :, j0 - g0 : j1 - g0])
 
         def middle(c):
+            j0, j1 = bounds[c], bounds[c + 1]
             codes, scales = quantise(z_woven[c], "z%d" % c)
-            passes(c, wb_dealt, 4, codes, scales, False)
-            y = keep.tile([P, PACK, CHUNK], F32, name="y%d" % c)
-            for h in range(CHUNK // BANK_J):
-                nc.scalar.copy(out=y[:, :, h * BANK_J : (h + 1) * BANK_J], in_=banks[c * (CHUNK // BANK_J) + h][:])
-            nc.sync.dma_start(out=y_rows[:, :, c * CHUNK : (c + 1) * CHUNK], in_=y[:])
+            passes(j0, j1, 1, codes, scales)
+            y = keep.tile([P, PACK, j1 - j0], F32, name="y%d" % c)
+            for b0 in range(j0, j1, BANK_J):
+                nc.scalar.copy(out=y[:, :, b0 - j0 : b0 - j0 + BANK_J], in_=banks[b0 // BANK_J][:])
+            nc.sync.dma_start(out=y_rows[:, :, j0:j1], in_=y[:])
             return y
 
         def back(c, y):
-            cols = slice(c * CHUNK, (c + 1) * CHUNK)
-            y_woven = keep.tile([P, CHUNK, PACK], BF16, name="y_woven%d" % c, align_bytes=64)
-            nc.vector.tensor_copy(
-                out=y_woven[:].rearrange("p (c r) t -> p c t r", r=4),
-                in_=y[:].rearrange("p t (c r) -> p c t r", r=4),
-            )
-            y_codes = keep.tile([P, CHUNK], I32, name="y_codes%d" % c, align_bytes=64)
+            j0, j1 = bounds[c], bounds[c + 1]
+            cols = slice(j0, j1)
+            y_woven = keep.tile([P, j1 - j0, PACK], BF16, name="y_woven%d" % c, align_bytes=64)
+            if c in SCALAR_ROUNDS:
+                for b0 in range(j0, j1, BANK_J):
+                    nc.scalar.copy(
+                        out=y_woven[:, b0 - j0 : b0 - j0 + BANK_J, :],
+                        in_=banks[b0 // BANK_J][:].rearrange("p t j -> p j t"),
+                    )
+            else:
+                weave(nc.vector.tensor_copy, y_woven[:], y[:])
+            y_codes = keep.tile([P, j1 - j0], I32, name="y_codes%d" % c, align_bytes=64)
             nc.vector.quantize_mx(
                 out=y_codes[:].bitcast(FP8X4), scales=y_scales[:, cols], in_=y_woven[:].rearrange("p j t -> p (j t)")
             )
             nc.sync.dma_start(out=y_words[:, cols], in_=y_codes[:])
 
         ys = {}
+        front(0)
         for s in range(n_chunks + 2):
-            if s < n_chunks:
-                front(s)
             if 1 <= s <= n_chunks:
                 ys[s - 1] = middle(s - 1)
+            if s + 1 < n_chunks:
+                front(s + 1)
             if s >= 2:
                 back(s - 2, ys[s - 2])
-        for q in range(4):
-            nc.sync.dma_start(
+        for q in range(QUADS):
+            queue = nc.sync if q % 2 == 0 else nc.scalar
+            queue.dma_start(
                 out=out_2[0, 4 * q : 4 * q + 4, :].bitcast(I32), in_=y_scales[32 * q : 32 * q + 4, :].bitcast(I32)
             )

@@ -17,10 +17,11 @@ MULT = mybir.AluOpType.mult
 P = 128
 PACK = 4
 BANK_J = 128
-X_CHUNK = 256
-Z_GROUPS = ((128, 256, 256), (256,), (128,))
-SCALAR_ROUNDS = (0, 1)
-VECTOR_WEAVES = (0, 3, 4)
+X_CHUNK = 512
+CODE_STORES = (2, 3)
+Z_GROUPS = (256, 256, 256, 256)
+SCALAR_ROUNDS = ()
+VECTOR_WEAVES = (3,)
 HOLD = 3
 X_STEPS = ((0, 1), (1, 2), (2, 4))
 LIST_ROWS = 16
@@ -44,51 +45,53 @@ def tile_list_sum_noneP_kernel(
         z_list = keep.tile([P, J // LIST_ROWS], U16, name="z_list")
         x_gain = keep.tile([P, J], F32, name="x_gain")
         z_gain = keep.tile([P, J], F32, name="z_gain")
-        x_gain_rows = keep.tile([P, J // QUADS], F32, name="x_gain_rows")
-        z_gain_rows = keep.tile([P, J // QUADS], F32, name="z_gain_rows")
         w_raw = keep.tile([P, 2, N], I32, name="w_raw")
-        ws_raw = keep.tile([P, N], U8, name="ws_raw")
+        ws_raw = keep.tile([P, N // 4], I32, name="ws_raw")
         identity = keep.tile([P, P], F32, name="identity")
 
-        nc.vector.memset(ws_raw[:].bitcast(I32), 0)
+        nc.vector.memset(ws_raw[:], 0)
         make_identity(nc, identity[:])
 
-        def load_scale_rows(q):
-            for first, scales in ((0, wa_scales), (4, wb_scales)):
+        def load_scale_rows(scales, first):
+            for q in range(QUADS):
                 nc.sync.dma_start(
-                    out=ws_raw[32 * q + first : 32 * q + first + 4, :].bitcast(I32),
+                    out=ws_raw[32 * q + first : 32 * q + first + 4, :],
                     in_=scales[0, 4 * q : 4 * q + 4, :].bitcast(I32),
                 )
 
-        def load_gain_rows(rows, gain_hbm):
-            width = J // QUADS
-            for q in range(QUADS):
-                nc.sync.dma_start(out=rows[32 * q : 32 * q + 32, :], in_=gain_hbm[0:P:4, q * width : (q + 1) * width])
+        def load_gain_rows(gain_hbm, parts, name):
+            width = J // parts
+            rows = keep.tile([P, width], F32, name=name)
+            for q in range(parts):
+                nc.sync.dma_start(
+                    out=rows[q * P // parts : (q + 1) * P // parts, :],
+                    in_=gain_hbm[0:P:parts, q * width : (q + 1) * width],
+                )
+            return rows
 
-        load_gain_rows(x_gain_rows, wgt)
+        x_gain_rows = load_gain_rows(wgt, 4, "x_gain_rows")
         nc.sync.dma_start(x_list[:], offs)
         nc.sync.dma_start(out=x_planes[0][:], in_=x_rows[:, 0, :])
         nc.sync.dma_start(out=x_planes[1][:], in_=x_rows[:, 1, :])
-        load_gain_rows(z_gain_rows, wgt2)
+        load_scale_rows(wa_scales, 0)
+        z_gain_rows = load_gain_rows(wgt2, 2, "z_gain_rows")
         nc.sync.dma_start(out=x_planes[2][:], in_=x_rows[:, 2, :])
-        load_scale_rows(0)
         nc.sync.dma_start(out=x_planes[3][:], in_=x_rows[:, 3, :])
-        load_scale_rows(1)
-        load_scale_rows(2)
+        load_scale_rows(wb_scales, 4)
         nc.sync.dma_start(out=w_raw[:, 0, :], in_=wa_words[0].rearrange("p n i -> p (n i)").bitcast(I32))
         nc.sync.dma_start(out=w_raw[:, 1, :], in_=wb_words[0].rearrange("p n i -> p (n i)").bitcast(I32))
         nc.sync.dma_start(out=z_planes[0][:], in_=z_rows[:, 0, :])
         nc.sync.dma_start(z_list[:], offs2)
-        load_scale_rows(3)
         for i in range(1, PACK):
             nc.sync.dma_start(out=z_planes[i][:], in_=z_rows[:, i, :])
 
-        def spread_gain(rows, gain, name, steps):
-            blocks = J // QUADS // P
+        def spread_gain(rows, gain, name, parts, steps):
+            width = J // parts
+            blocks = width // P
             turned = psum.tile([P, blocks, P], F32, name=name + "_turned", tag="bank7")
             for b in range(blocks):
                 nc.tensor.transpose(turned[:, b, :], rows[:, b * P : (b + 1) * P], identity[:])
-            by_place = turned[:].rearrange("p b (q g s) -> p q b g s", q=QUADS, g=HEADS)
+            by_place = turned[:].rearrange("p b (q g s) -> p q b g s", q=parts, g=HEADS)
             for q0, q1 in steps:
                 wide = keep.tile([P, q1 - q0, blocks, HEADS, LIST_ROWS], F32, name=name + "_wide%d" % q0)
                 nc.scalar.copy(
@@ -100,11 +103,11 @@ def tile_list_sum_noneP_kernel(
                 for u in range((q1 - q0) * blocks):
                     nc.tensor.transpose(back[:, u, :], flat[:, u, :], identity[:])
                 nc.scalar.copy(
-                    out=gain[:, q0 * (J // QUADS) : q1 * (J // QUADS)], in_=back[:].rearrange("p u r -> p (u r)")
+                    out=gain[:, q0 * width : q1 * width], in_=back[:].rearrange("p u r -> p (u r)")
                 )
 
-        spread_gain(x_gain_rows, x_gain, "x_gain", X_STEPS)
-        spread_gain(z_gain_rows, z_gain, "z_gain", ((0, 2), (2, 4)))
+        spread_gain(x_gain_rows, x_gain, "x_gain", 4, X_STEPS)
+        spread_gain(z_gain_rows, z_gain, "z_gain", 2, ((0, 1), (1, 2)))
 
         def gather(picked, plane, offsets, gain, j0, j1):
             nc.vector.tensor_tensor(
@@ -159,35 +162,39 @@ def tile_list_sum_noneP_kernel(
             gather(x_picked[:, PACK - 1, j0:j1], x_planes[PACK - 1], x_list, x_gain, j0, j1)
             x_woven[j0] = keep.tile([P, X_CHUNK, PACK], BF16, name="x_woven%d" % j0, align_bytes=64)
             weave(nc.scalar.copy, x_woven[j0][:], x_picked[:, :, j0:j1])
-        nc.vector.tensor_copy(out=ws_dealt[:], in_=ws_raw[:].rearrange("p (m t) -> p t m", t=PACK))
+        nc.vector.tensor_copy(out=ws_dealt[:], in_=ws_raw[:].bitcast(U8).rearrange("p (m t) -> p t m", t=PACK))
         for j0 in range(0, J, X_CHUNK):
             codes, scales = quantise(x_woven[j0], "x%d" % j0)
             passes(j0, j0 + X_CHUNK, 0, codes, scales)
 
-        widths = [w for group in Z_GROUPS for w in group]
+        widths = Z_GROUPS
         bounds = [sum(widths[:c]) for c in range(len(widths) + 1)]
         n_chunks = len(widths)
-        group_of = [g for g, group in enumerate(Z_GROUPS) for w in group]
-        z_woven = {}
-        z_picked = {}
+        z_woven = [
+            keep.tile([P, widths[c], PACK], BF16, name="z_woven%d" % c, tag="z_woven%d" % c, align_bytes=64)
+            for c in range(n_chunks)
+        ]
+        z_low = keep.tile([P, 2, J], F32, name="z_low")
+        gather(z_low[:, 0, :], z_planes[0], z_list, z_gain, 0, J)
+        for j0 in range(0, J, J // 2):
+            gather(z_low[:, 1, j0 : j0 + J // 2], z_planes[1], z_list, z_gain, j0, j0 + J // 2)
+        for c in range(n_chunks):
+            nc.scalar.copy(
+                out=z_woven[c][:, :, 0:2], in_=z_low[:, :, bounds[c] : bounds[c + 1]].rearrange("p i j -> p j i")
+            )
 
         y_rows = out_0.rearrange("(p t) j -> p t j", t=PACK)
         y_words = out_1[0].rearrange("p j i -> p (j i)").bitcast(I32)
+        y_codes = keep.tile([P, J], I32, name="y_codes", align_bytes=64)
         y_scales = keep.tile([P, J], U8, name="y_scales", align_bytes=64)
 
         def front(c):
-            g = group_of[c]
-            first = group_of.index(g)
-            g0, g1 = bounds[first], bounds[first] + sum(Z_GROUPS[g])
-            j0, j1 = bounds[c], bounds[c + 1]
-            if c == first:
-                tag = "z_woven%d" % (c - HOLD) if g > 0 else "z_first"
-                z_picked[g] = keep.tile([P, PACK, g1 - g0], F32, name="z_picked%d" % g, tag=tag, align_bytes=64)
-                for i in range(PACK - 1):
-                    gather(z_picked[g][:, i, :], z_planes[i], z_list, z_gain, g0, g1)
-            gather(z_picked[g][:, PACK - 1, j0 - g0 : j1 - g0], z_planes[PACK - 1], z_list, z_gain, j0, j1)
-            z_woven[c] = keep.tile([P, j1 - j0, PACK], BF16, name="z_woven%d" % c, tag="z_woven%d" % c, align_bytes=64)
-            weave(nc.vector.tensor_copy if c in VECTOR_WEAVES else nc.scalar.copy, z_woven[c][:], z_picked[g][:, :, j0 - g0 : j1 - g0])
+            tag = "z_woven%d" % (c - HOLD) if c >= HOLD else "z_high%d" % c
+            z_high = keep.tile([P, 2, widths[c]], F32, name="z_high%d" % c, tag=tag, align_bytes=64)
+            for i in range(2):
+                gather(z_high[:, i, :], z_planes[2 + i], z_list, z_gain, bounds[c], bounds[c + 1])
+            engine_copy = nc.vector.tensor_copy if c in VECTOR_WEAVES else nc.scalar.copy
+            engine_copy(out=z_woven[c][:, :, 2:4], in_=z_high[:].rearrange("p i j -> p j i"))
 
         def middle(c):
             j0, j1 = bounds[c], bounds[c + 1]
@@ -211,11 +218,12 @@ def tile_list_sum_noneP_kernel(
                     )
             else:
                 weave(nc.vector.tensor_copy, y_woven[:], y[:])
-            y_codes = keep.tile([P, j1 - j0], I32, name="y_codes%d" % c, align_bytes=64)
             nc.vector.quantize_mx(
-                out=y_codes[:].bitcast(FP8X4), scales=y_scales[:, cols], in_=y_woven[:].rearrange("p j t -> p (j t)")
+                out=y_codes[:, cols].bitcast(FP8X4), scales=y_scales[:, cols], in_=y_woven[:].rearrange("p j t -> p (j t)")
             )
-            nc.sync.dma_start(out=y_words[:, cols], in_=y_codes[:])
+            if c in CODE_STORES:
+                done = slice(bounds[max([k for k in CODE_STORES if k < c] + [-1]) + 1], j1)
+                nc.sync.dma_start(out=y_words[:, done], in_=y_codes[:, done])
 
         ys = {}
         front(0)

@@ -116,7 +116,7 @@ def tile_list_sum_noneP_kernel(
 
         def weave(engine_copy, woven, planes):
             engine_copy(
-                out=woven.rearrange("p (c r) i -> p c i r", r=4), in_=planes.rearrange("p i (c r) -> p c i r", r=4)
+                out=woven.rearrange("p (c r) i -> p c i r", r=2), in_=planes.rearrange("p i (c r) -> p c i r", r=2)
             )
 
         def quantise(woven, name):

@@ -16,17 +16,18 @@ MULT = mybir.AluOpType.mult
 
 P = 128
 PACK = 4
-BANK_J = 128
-X_CHUNK = 512
-CODE_STORES = (2, 3)
-Z_GROUPS = (256, 256, 256, 256)
-SCALAR_ROUNDS = ()
-VECTOR_WEAVES = (3,)
-HOLD = 3
-X_STEPS = ((0, 1), (1, 2), (2, 4))
-LIST_ROWS = 16
-QUADS = 4
 HEADS = 8
+HEAD_ROWS = P // HEADS
+QUADRANTS = 4
+BANK_J = 128
+HALF = J // 2
+CHUNK = 256
+CHUNKS = J // CHUNK
+LAST = CHUNKS - 1
+X_GAIN_PARTS = 4
+Z_GAIN_PARTS = 2
+X_GAIN_STEPS = ((0, 1), (1, 2), (2, 4))
+Z_GAIN_STEPS = ((0, 1), (1, 2))
 
 
 def tile_list_sum_noneP_kernel(
@@ -41,21 +42,21 @@ def tile_list_sum_noneP_kernel(
         z_rows = zT.rearrange("(p i) t -> p i t", i=PACK)
         x_planes = [keep.tile([P, T], F32, name="x_plane%d" % i) for i in range(PACK)]
         z_planes = [keep.tile([P, T], F32, name="z_plane%d" % i) for i in range(PACK)]
-        x_list = keep.tile([P, J // LIST_ROWS], U16, name="x_list")
-        z_list = keep.tile([P, J // LIST_ROWS], U16, name="z_list")
+        x_list = keep.tile([P, J // HEAD_ROWS], U16, name="x_list")
+        z_list = keep.tile([P, J // HEAD_ROWS], U16, name="z_list")
         x_gain = keep.tile([P, J], F32, name="x_gain")
         z_gain = keep.tile([P, J], F32, name="z_gain")
         w_raw = keep.tile([P, 2, N], I32, name="w_raw")
-        ws_raw = keep.tile([P, N // 4], I32, name="ws_raw")
+        w_scales_raw = keep.tile([P, N // 4], I32, name="w_scales_raw")
         identity = keep.tile([P, P], F32, name="identity")
 
-        nc.vector.memset(ws_raw[:], 0)
+        nc.vector.memset(w_scales_raw[:], 0)
         make_identity(nc, identity[:])
 
         def load_scale_rows(scales, first):
-            for q in range(QUADS):
+            for q in range(QUADRANTS):
                 nc.sync.dma_start(
-                    out=ws_raw[32 * q + first : 32 * q + first + 4, :],
+                    out=w_scales_raw[32 * q + first : 32 * q + first + 4, :],
                     in_=scales[0, 4 * q : 4 * q + 4, :].bitcast(I32),
                 )
 
@@ -69,12 +70,12 @@ def tile_list_sum_noneP_kernel(
                 )
             return rows
 
-        x_gain_rows = load_gain_rows(wgt, 4, "x_gain_rows")
+        x_gain_rows = load_gain_rows(wgt, X_GAIN_PARTS, "x_gain_rows")
         nc.sync.dma_start(x_list[:], offs)
         nc.sync.dma_start(out=x_planes[0][:], in_=x_rows[:, 0, :])
         nc.sync.dma_start(out=x_planes[1][:], in_=x_rows[:, 1, :])
         load_scale_rows(wa_scales, 0)
-        z_gain_rows = load_gain_rows(wgt2, 2, "z_gain_rows")
+        z_gain_rows = load_gain_rows(wgt2, Z_GAIN_PARTS, "z_gain_rows")
         nc.sync.dma_start(out=x_planes[2][:], in_=x_rows[:, 2, :])
         nc.sync.dma_start(out=x_planes[3][:], in_=x_rows[:, 3, :])
         load_scale_rows(wb_scales, 4)
@@ -93,25 +94,21 @@ def tile_list_sum_noneP_kernel(
                 nc.tensor.transpose(turned[:, b, :], rows[:, b * P : (b + 1) * P], identity[:])
             by_place = turned[:].rearrange("p b (q g s) -> p q b g s", q=parts, g=HEADS)
             for q0, q1 in steps:
-                wide = keep.tile([P, q1 - q0, blocks, HEADS, LIST_ROWS], F32, name=name + "_wide%d" % q0)
-                nc.scalar.copy(
-                    out=wide[:],
-                    in_=by_place[:, q0:q1, :, :, 0:1].to_broadcast([P, q1 - q0, blocks, HEADS, LIST_ROWS]),
-                )
+                shape = [P, q1 - q0, blocks, HEADS, HEAD_ROWS]
+                wide = keep.tile(shape, F32, name=name + "_wide%d" % q0)
+                nc.scalar.copy(out=wide[:], in_=by_place[:, q0:q1, :, :, 0:1].to_broadcast(shape))
                 back = psum.tile([P, (q1 - q0) * blocks, P], F32, name=name + "_back%d" % q0, tag="bank%d" % (3 + q0))
                 flat = wide[:].rearrange("p q b g s -> p (q b) (g s)")
                 for u in range((q1 - q0) * blocks):
                     nc.tensor.transpose(back[:, u, :], flat[:, u, :], identity[:])
-                nc.scalar.copy(
-                    out=gain[:, q0 * width : q1 * width], in_=back[:].rearrange("p u r -> p (u r)")
-                )
+                nc.scalar.copy(out=gain[:, q0 * width : q1 * width], in_=back[:].rearrange("p u r -> p (u r)"))
 
-        spread_gain(x_gain_rows, x_gain, "x_gain", 4, X_STEPS)
-        spread_gain(z_gain_rows, z_gain, "z_gain", 2, ((0, 1), (1, 2)))
+        spread_gain(x_gain_rows, x_gain, "x_gain", X_GAIN_PARTS, X_GAIN_STEPS)
+        spread_gain(z_gain_rows, z_gain, "z_gain", Z_GAIN_PARTS, Z_GAIN_STEPS)
 
         def gather(picked, plane, offsets, gain, j0, j1):
             nc.vector.tensor_tensor(
-                picked, plane[:].indirect(offsets[:, j0 // LIST_ROWS : j1 // LIST_ROWS]), gain[:, j0:j1], MULT
+                picked, plane[:].indirect(offsets[:, j0 // HEAD_ROWS : j1 // HEAD_ROWS]), gain[:, j0:j1], MULT
             )
 
         def weave(engine_copy, woven, planes):
@@ -130,7 +127,7 @@ def tile_list_sum_noneP_kernel(
 
         banks = [psum.tile([P, PACK, BANK_J], F32, name="bank%d" % b, tag="bank%d" % b) for b in range(J // BANK_J)]
         w_dealt = keep.tile([P, 2, PACK, P], I32, name="w_dealt", align_bytes=64)
-        ws_dealt = keep.tile([P, PACK, P], U8, name="ws_dealt", align_bytes=64)
+        w_scales_dealt = keep.tile([P, PACK, P], U8, name="w_scales_dealt", align_bytes=64)
 
         def passes(j0, j1, stream, codes, scales):
             for b0 in range(j0, j1, BANK_J):
@@ -139,7 +136,7 @@ def tile_list_sum_noneP_kernel(
                     nc.tensor.matmul_mx(
                         out=banks[b0 // BANK_J][:, t, :],
                         lhsT=w_dealt[:, stream, t, :].bitcast(FP8X4),
-                        lhsT_scale=ws_dealt[4 * stream : P, t, :],
+                        lhsT_scale=w_scales_dealt[4 * stream : P, t, :],
                         rhs=codes[:, cols].bitcast(FP8X4),
                         rhs_scale=scales[:, cols],
                         start=(stream == 0 and t == 0),
@@ -147,8 +144,8 @@ def tile_list_sum_noneP_kernel(
                     )
 
         x_picked = keep.tile([P, PACK, J], F32, name="x_picked")
-        for q0, q1 in X_STEPS:
-            j0, j1 = q0 * (J // QUADS), q1 * (J // QUADS)
+        for q0, q1 in X_GAIN_STEPS:
+            j0, j1 = q0 * J // X_GAIN_PARTS, q1 * J // X_GAIN_PARTS
             gather(x_picked[:, 0, j0:j1], x_planes[0], x_list, x_gain, j0, j1)
         for i in range(1, PACK - 1):
             gather(x_picked[:, i, :], x_planes[i], x_list, x_gain, 0, J)
@@ -157,84 +154,83 @@ def tile_list_sum_noneP_kernel(
             in_=w_raw[:].rearrange("p w (a r t) -> p w a t r", r=4, t=PACK),
         )
         x_woven = {}
-        for j0 in range(0, J, X_CHUNK):
-            j1 = j0 + X_CHUNK
-            gather(x_picked[:, PACK - 1, j0:j1], x_planes[PACK - 1], x_list, x_gain, j0, j1)
-            x_woven[j0] = keep.tile([P, X_CHUNK, PACK], BF16, name="x_woven%d" % j0, align_bytes=64)
-            weave(nc.scalar.copy, x_woven[j0][:], x_picked[:, :, j0:j1])
-        nc.vector.tensor_copy(out=ws_dealt[:], in_=ws_raw[:].bitcast(U8).rearrange("p (m t) -> p t m", t=PACK))
-        for j0 in range(0, J, X_CHUNK):
+        for j0 in range(0, J, HALF):
+            gather(x_picked[:, PACK - 1, j0 : j0 + HALF], x_planes[PACK - 1], x_list, x_gain, j0, j0 + HALF)
+            x_woven[j0] = keep.tile([P, HALF, PACK], BF16, name="x_woven%d" % j0, align_bytes=64)
+            weave(nc.scalar.copy, x_woven[j0][:], x_picked[:, :, j0 : j0 + HALF])
+        nc.vector.tensor_copy(
+            out=w_scales_dealt[:], in_=w_scales_raw[:].bitcast(U8).rearrange("p (m t) -> p t m", t=PACK)
+        )
+        for j0 in range(0, J, HALF):
             codes, scales = quantise(x_woven[j0], "x%d" % j0)
-            passes(j0, j0 + X_CHUNK, 0, codes, scales)
+            passes(j0, j0 + HALF, 0, codes, scales)
 
-        widths = Z_GROUPS
-        bounds = [sum(widths[:c]) for c in range(len(widths) + 1)]
-        n_chunks = len(widths)
         z_woven = [
-            keep.tile([P, widths[c], PACK], BF16, name="z_woven%d" % c, tag="z_woven%d" % c, align_bytes=64)
-            for c in range(n_chunks)
+            keep.tile([P, CHUNK, PACK], BF16, name="z_woven%d" % c, tag="z_woven%d" % c, align_bytes=64)
+            for c in range(CHUNKS)
         ]
         z_low = keep.tile([P, 2, J], F32, name="z_low")
         gather(z_low[:, 0, :], z_planes[0], z_list, z_gain, 0, J)
-        for j0 in range(0, J, J // 2):
-            gather(z_low[:, 1, j0 : j0 + J // 2], z_planes[1], z_list, z_gain, j0, j0 + J // 2)
-        for c in range(n_chunks):
+        for j0 in range(0, J, HALF):
+            gather(z_low[:, 1, j0 : j0 + HALF], z_planes[1], z_list, z_gain, j0, j0 + HALF)
+        for c in range(CHUNKS):
             nc.scalar.copy(
-                out=z_woven[c][:, :, 0:2], in_=z_low[:, :, bounds[c] : bounds[c + 1]].rearrange("p i j -> p j i")
+                out=z_woven[c][:, :, 0:2], in_=z_low[:, :, c * CHUNK : (c + 1) * CHUNK].rearrange("p i j -> p j i")
             )
 
         y_rows = out_0.rearrange("(p t) j -> p t j", t=PACK)
         y_words = out_1[0].rearrange("p j i -> p (j i)").bitcast(I32)
         y_codes = keep.tile([P, J], I32, name="y_codes", align_bytes=64)
         y_scales = keep.tile([P, J], U8, name="y_scales", align_bytes=64)
+        y = {}
+        y_woven = {}
 
-        def front(c):
-            tag = "z_woven%d" % (c - HOLD) if c >= HOLD else "z_high%d" % c
-            z_high = keep.tile([P, 2, widths[c]], F32, name="z_high%d" % c, tag=tag, align_bytes=64)
+        def pick_high_planes(c):
+            tag = "z_woven0" if c == LAST else "z_high%d" % c
+            z_high = keep.tile([P, 2, CHUNK], F32, name="z_high%d" % c, tag=tag, align_bytes=64)
             for i in range(2):
-                gather(z_high[:, i, :], z_planes[2 + i], z_list, z_gain, bounds[c], bounds[c + 1])
-            engine_copy = nc.vector.tensor_copy if c in VECTOR_WEAVES else nc.scalar.copy
+                gather(z_high[:, i, :], z_planes[2 + i], z_list, z_gain, c * CHUNK, (c + 1) * CHUNK)
+            engine_copy = nc.vector.tensor_copy if c == LAST else nc.scalar.copy
             engine_copy(out=z_woven[c][:, :, 2:4], in_=z_high[:].rearrange("p i j -> p j i"))
 
-        def middle(c):
-            j0, j1 = bounds[c], bounds[c + 1]
+        def finish_sums(c):
+            j0, j1 = c * CHUNK, (c + 1) * CHUNK
             codes, scales = quantise(z_woven[c], "z%d" % c)
             passes(j0, j1, 1, codes, scales)
-            y = keep.tile([P, PACK, j1 - j0], F32, name="y%d" % c)
+            y[c] = keep.tile([P, PACK, CHUNK], F32, name="y%d" % c)
+            y_woven[c] = keep.tile([P, CHUNK, PACK], BF16, name="y_woven%d" % c, align_bytes=64)
             for b0 in range(j0, j1, BANK_J):
-                nc.scalar.copy(out=y[:, :, b0 - j0 : b0 - j0 + BANK_J], in_=banks[b0 // BANK_J][:])
-            nc.sync.dma_start(out=y_rows[:, :, j0:j1], in_=y[:])
-            return y
-
-        def back(c, y):
-            j0, j1 = bounds[c], bounds[c + 1]
-            cols = slice(j0, j1)
-            y_woven = keep.tile([P, j1 - j0, PACK], BF16, name="y_woven%d" % c, align_bytes=64)
-            if c in SCALAR_ROUNDS:
+                nc.scalar.copy(out=y[c][:, :, b0 - j0 : b0 - j0 + BANK_J], in_=banks[b0 // BANK_J][:])
+            nc.sync.dma_start(out=y_rows[:, :, j0:j1], in_=y[c][:])
+            if c == LAST:
                 for b0 in range(j0, j1, BANK_J):
                     nc.scalar.copy(
-                        out=y_woven[:, b0 - j0 : b0 - j0 + BANK_J, :],
+                        out=y_woven[c][:, b0 - j0 : b0 - j0 + BANK_J, :],
                         in_=banks[b0 // BANK_J][:].rearrange("p t j -> p j t"),
                     )
-            else:
-                weave(nc.vector.tensor_copy, y_woven[:], y[:])
-            nc.vector.quantize_mx(
-                out=y_codes[:, cols].bitcast(FP8X4), scales=y_scales[:, cols], in_=y_woven[:].rearrange("p j t -> p (j t)")
-            )
-            if c in CODE_STORES:
-                done = slice(bounds[max([k for k in CODE_STORES if k < c] + [-1]) + 1], j1)
-                nc.sync.dma_start(out=y_words[:, done], in_=y_codes[:, done])
 
-        ys = {}
-        front(0)
-        for s in range(n_chunks + 2):
-            if 1 <= s <= n_chunks:
-                ys[s - 1] = middle(s - 1)
-            if s + 1 < n_chunks:
-                front(s + 1)
+        def quantise_result(c):
+            j0, j1 = c * CHUNK, (c + 1) * CHUNK
+            if c != LAST:
+                weave(nc.vector.tensor_copy, y_woven[c][:], y[c][:])
+            nc.vector.quantize_mx(
+                out=y_codes[:, j0:j1].bitcast(FP8X4),
+                scales=y_scales[:, j0:j1],
+                in_=y_woven[c][:].rearrange("p j t -> p (j t)"),
+            )
+            if j1 % HALF == 0:
+                nc.sync.dma_start(out=y_words[:, j1 - HALF : j1], in_=y_codes[:, j1 - HALF : j1])
+
+        pick_high_planes(0)
+        for s in range(CHUNKS + 2):
+            if 1 <= s <= CHUNKS:
+                finish_sums(s - 1)
+            if s + 1 < CHUNKS:
+                pick_high_planes(s + 1)
             if s >= 2:
-                back(s - 2, ys[s - 2])
-        for q in range(QUADS):
+                quantise_result(s - 2)
+
+        for q in range(QUADRANTS):
             queue = nc.sync if q % 2 == 0 else nc.scalar
             queue.dma_start(
                 out=out_2[0, 4 * q : 4 * q + 4, :].bitcast(I32), in_=y_scales[32 * q : 32 * q + 4, :].bitcast(I32)

from contextlib import ExitStack

import concourse.mybir as mybir
from concourse.masks import make_identity

K, L, N, T, J = 512, 512, 512, 2048, 1024
FLOPS = 2 * (K + L) * N * J

F32 = mybir.dt.float32
BF16 = mybir.dt.bfloat16
I32 = mybir.dt.int32
U16 = mybir.dt.uint16
U8 = mybir.dt.uint8
FP8X4 = mybir.dt.float8_e4m3fn_x4
MULT = mybir.AluOpType.mult

P = 128
PACK = 4
HEADS = 8
HEAD_ROWS = P // HEADS
QUADRANTS = 4
BANK_J = 128
HALF = J // 2
CHUNK = 256
CHUNKS = J // CHUNK
LAST = CHUNKS - 1
X_GAIN_PARTS = 4
Z_GAIN_PARTS = 2
X_GAIN_STEPS = ((0, 1), (1, 2), (2, 4))
Z_GAIN_STEPS = ((0, 1), (1, 2))


def tile_list_sum_noneP_kernel(
    tc, xT, wgt, zT, wgt2, wa_words, wa_scales, wb_words, wb_scales, offs, offs2, out_0, out_1, out_2
):
    nc = tc.nc
    with ExitStack() as ctx:
        keep = ctx.enter_context(tc.tile_pool(name="keep", bufs=1))
        psum = ctx.enter_context(tc.psum_pool(name="psum", bufs=1))

        x_rows = xT.rearrange("(p i) t -> p i t", i=PACK)
        z_rows = zT.rearrange("(p i) t -> p i t", i=PACK)
        x_planes = [keep.tile([P, T], F32, name="x_plane%d" % i) for i in range(PACK)]
        z_planes = [keep.tile([P, T], F32, name="z_plane%d" % i) for i in range(PACK)]
        x_list = keep.tile([P, J // HEAD_ROWS], U16, name="x_list")
        z_list = keep.tile([P, J // HEAD_ROWS], U16, name="z_list")
        x_gain = keep.tile([P, J], F32, name="x_gain")
        z_gain = keep.tile([P, J], F32, name="z_gain")
        w_raw = keep.tile([P, 2, N], I32, name="w_raw")
        w_scales_raw = keep.tile([P, N // 4], I32, name="w_scales_raw")
        identity = keep.tile([P, P], F32, name="identity")

        nc.vector.memset(w_scales_raw[:], 0)
        make_identity(nc, identity[:])

        def load_scale_rows(scales, first):
            for q in range(QUADRANTS):
                nc.sync.dma_start(
                    out=w_scales_raw[32 * q + first : 32 * q + first + 4, :],
                    in_=scales[0, 4 * q : 4 * q + 4, :].bitcast(I32),
                )

        def load_gain_rows(gain_hbm, parts, name):
            width = J // parts
            rows = keep.tile([P, width], F32, name=name)
            for q in range(parts):
                nc.sync.dma_start(
                    out=rows[q * P // parts : (q + 1) * P // parts, :],
                    in_=gain_hbm[0:P:parts, q * width : (q + 1) * width],
                )
            return rows

        x_gain_rows = load_gain_rows(wgt, X_GAIN_PARTS, "x_gain_rows")
        nc.sync.dma_start(x_list[:], offs)
        nc.sync.dma_start(out=x_planes[0][:], in_=x_rows[:, 0, :])
        nc.sync.dma_start(out=x_planes[1][:], in_=x_rows[:, 1, :])
        load_scale_rows(wa_scales, 0)
        z_gain_rows = load_gain_rows(wgt2, Z_GAIN_PARTS, "z_gain_rows")
        nc.sync.dma_start(out=x_planes[2][:], in_=x_rows[:, 2, :])
        nc.sync.dma_start(out=x_planes[3][:], in_=x_rows[:, 3, :])
        load_scale_rows(wb_scales, 4)
        nc.sync.dma_start(out=w_raw[:, 0, :], in_=wa_words[0].rearrange("p n i -> p (n i)").bitcast(I32))
        nc.sync.dma_start(out=w_raw[:, 1, :], in_=wb_words[0].rearrange("p n i -> p (n i)").bitcast(I32))
        nc.sync.dma_start(out=z_planes[0][:], in_=z_rows[:, 0, :])
        nc.sync.dma_start(z_list[:], offs2)
        for i in range(1, PACK):
            nc.sync.dma_start(out=z_planes[i][:], in_=z_rows[:, i, :])

        def spread_gain(rows, gain, name, parts, steps):
            width = J // parts
            blocks = width // P
            turned = psum.tile([P, blocks, P], F32, name=name + "_turned", tag="bank7")
            for b in range(blocks):
                nc.tensor.transpose(turned[:, b, :], rows[:, b * P : (b + 1) * P], identity[:])
            by_place = turned[:].rearrange("p b (q g s) -> p q b g s", q=parts, g=HEADS)
            for q0, q1 in steps:
                shape = [P, q1 - q0, blocks, HEADS, HEAD_ROWS]
                wide = keep.tile(shape, F32, name=name + "_wide%d" % q0)
                nc.scalar.copy(out=wide[:], in_=by_place[:, q0:q1, :, :, 0:1].to_broadcast(shape))
                back = psum.tile([P, (q1 - q0) * blocks, P], F32, name=name + "_back%d" % q0, tag="bank%d" % (3 + q0))
                flat = wide[:].rearrange("p q b g s -> p (q b) (g s)")
                for u in range((q1 - q0) * blocks):
                    nc.tensor.transpose(back[:, u, :], flat[:, u, :], identity[:])
                nc.scalar.copy(out=gain[:, q0 * width : q1 * width], in_=back[:].rearrange("p u r -> p (u r)"))

        spread_gain(x_gain_rows, x_gain, "x_gain", X_GAIN_PARTS, X_GAIN_STEPS)
        spread_gain(z_gain_rows, z_gain, "z_gain", Z_GAIN_PARTS, Z_GAIN_STEPS)

        def gather(picked, plane, offsets, gain, j0, j1):
            nc.vector.tensor_tensor(
                picked, plane[:].indirect(offsets[:, j0 // HEAD_ROWS : j1 // HEAD_ROWS]), gain[:, j0:j1], MULT
            )

        def weave(engine_copy, woven, planes):
            engine_copy(
                out=woven.rearrange("p (c r) i -> p c i r", r=2), in_=planes.rearrange("p i (c r) -> p c i r", r=2)
            )

        def quantise(woven, name):
            width = woven.shape[1]
            codes = keep.tile([P, width], I32, name=name + "_codes", align_bytes=64)
            scales = keep.tile([P, width], U8, name=name + "_scales", align_bytes=64)
            nc.vector.quantize_mx(
                out=codes[:].bitcast(FP8X4), scales=scales[:], in_=woven[:].rearrange("p j i -> p (j i)")
            )
            return codes, scales

        banks = [psum.tile([P, PACK, BANK_J], F32, name="bank%d" % b, tag="bank%d" % b) for b in range(J // BANK_J)]
        w_dealt = keep.tile([P, 2, PACK, P], I32, name="w_dealt", align_bytes=64)
        w_scales_dealt = keep.tile([P, PACK, P], U8, name="w_scales_dealt", align_bytes=64)

        def passes(j0, j1, stream, codes, scales):
            for b0 in range(j0, j1, BANK_J):
                cols = slice(b0 - j0, b0 - j0 + BANK_J)
                for t in range(PACK):
                    nc.tensor.matmul_mx(
                        out=banks[b0 // BANK_J][:, t, :],
                        lhsT=w_dealt[:, stream, t, :].bitcast(FP8X4),
                        lhsT_scale=w_scales_dealt[4 * stream : P, t, :],
                        rhs=codes[:, cols].bitcast(FP8X4),
                        rhs_scale=scales[:, cols],
                        start=(stream == 0 and t == 0),
                        stop=(stream == 1 and t == PACK - 1),
                    )

        x_picked = keep.tile([P, PACK, J], F32, name="x_picked")
        for q0, q1 in X_GAIN_STEPS:
            j0, j1 = q0 * J // X_GAIN_PARTS, q1 * J // X_GAIN_PARTS
            gather(x_picked[:, 0, j0:j1], x_planes[0], x_list, x_gain, j0, j1)
        for i in range(1, PACK - 1):
            gather(x_picked[:, i, :], x_planes[i], x_list, x_gain, 0, J)
        nc.vector.tensor_copy(
            out=w_dealt[:].rearrange("p w t (a r) -> p w a t r", r=4),
            in_=w_raw[:].rearrange("p w (a r t) -> p w a t r", r=4, t=PACK),
        )
        x_woven = {}
        for j0 in range(0, J, HALF):
            gather(x_picked[:, PACK - 1, j0 : j0 + HALF], x_planes[PACK - 1], x_list, x_gain, j0, j0 + HALF)
            x_woven[j0] = keep.tile([P, HALF, PACK], BF16, name="x_woven%d" % j0, align_bytes=64)
            weave(nc.scalar.copy, x_woven[j0][:], x_picked[:, :, j0 : j0 + HALF])
        nc.vector.tensor_copy(
            out=w_scales_dealt[:], in_=w_scales_raw[:].bitcast(U8).rearrange("p (m t) -> p t m", t=PACK)
        )
        for j0 in range(0, J, HALF):
            codes, scales = quantise(x_woven[j0], "x%d" % j0)
            passes(j0, j0 + HALF, 0, codes, scales)

        z_woven = [
            keep.tile([P, CHUNK, PACK], BF16, name="z_woven%d" % c, tag="z_woven%d" % c, align_bytes=64)
            for c in range(CHUNKS)
        ]
        z_low = keep.tile([P, 2, J], F32, name="z_low")
        gather(z_low[:, 0, :], z_planes[0], z_list, z_gain, 0, J)
        for j0 in range(0, J, HALF):
            gather(z_low[:, 1, j0 : j0 + HALF], z_planes[1], z_list, z_gain, j0, j0 + HALF)
        for c in range(CHUNKS):
            nc.scalar.copy(
                out=z_woven[c][:, :, 0:2], in_=z_low[:, :, c * CHUNK : (c + 1) * CHUNK].rearrange("p i j -> p j i")
            )

        y_rows = out_0.rearrange("(p t) j -> p t j", t=PACK)
        y_words = out_1[0].rearrange("p j i -> p (j i)").bitcast(I32)
        y_codes = keep.tile([P, J], I32, name="y_codes", align_bytes=64)
        y_scales = keep.tile([P, J], U8, name="y_scales", align_bytes=64)
        y = {}
        y_woven = {}

        def pick_high_planes(c):
            tag = "z_woven0" if c == LAST else "z_high%d" % c
            z_high = keep.tile([P, 2, CHUNK], F32, name="z_high%d" % c, tag=tag, align_bytes=64)
            for i in range(2):
                gather(z_high[:, i, :], z_planes[2 + i], z_list, z_gain, c * CHUNK, (c + 1) * CHUNK)
            engine_copy = nc.vector.tensor_copy if c == LAST else nc.scalar.copy
            engine_copy(out=z_woven[c][:, :, 2:4], in_=z_high[:].rearrange("p i j -> p j i"))

        def finish_sums(c):
            j0, j1 = c * CHUNK, (c + 1) * CHUNK
            codes, scales = quantise(z_woven[c], "z%d" % c)
            passes(j0, j1, 1, codes, scales)
            y[c] = keep.tile([P, PACK, CHUNK], F32, name="y%d" % c)
            y_woven[c] = keep.tile([P, CHUNK, PACK], BF16, name="y_woven%d" % c, align_bytes=64)
            for b0 in range(j0, j1, BANK_J):
                nc.scalar.copy(out=y[c][:, :, b0 - j0 : b0 - j0 + BANK_J], in_=banks[b0 // BANK_J][:])
            nc.sync.dma_start(out=y_rows[:, :, j0:j1], in_=y[c][:])
            if c == LAST:
                for b0 in range(j0, j1, BANK_J):
                    nc.scalar.copy(
                        out=y_woven[c][:, b0 - j0 : b0 - j0 + BANK_J, :],
                        in_=banks[b0 // BANK_J][:].rearrange("p t j -> p j t"),
                    )

        def quantise_result(c):
            j0, j1 = c * CHUNK, (c + 1) * CHUNK
            if c != LAST:
                weave(nc.vector.tensor_copy, y_woven[c][:], y[c][:])
            nc.vector.quantize_mx(
                out=y_codes[:, j0:j1].bitcast(FP8X4),
                scales=y_scales[:, j0:j1],
                in_=y_woven[c][:].rearrange("p j t -> p (j t)"),
            )
            if j1 % HALF == 0:
                nc.sync.dma_start(out=y_words[:, j1 - HALF : j1], in_=y_codes[:, j1 - HALF : j1])

        pick_high_planes(0)
        for s in range(CHUNKS + 2):
            if 1 <= s <= CHUNKS:
                finish_sums(s - 1)
            if s + 1 < CHUNKS:
                pick_high_planes(s + 1)
            if s >= 2:
                quantise_result(s - 2)

        for q in range(QUADRANTS):
            queue = nc.sync if q % 2 == 0 else nc.scalar
            queue.dma_start(
                out=out_2[0, 4 * q : 4 * q + 4, :].bitcast(I32), in_=y_scales[32 * q : 32 * q + 4, :].bitcast(I32)
            )
